import numpy as np
import ml_dtypes


def mxq(x, axis, fmt="e4m3"):
    dtype, down = {"e4m3": (ml_dtypes.float8_e4m3fn, 7), "e5m2": (ml_dtypes.float8_e5m2, 14)}[fmt]
    v = np.moveaxis(np.asarray(x, np.float32).astype(ml_dtypes.bfloat16).astype(np.float64), axis, -1)
    blocks = v.reshape(v.shape[:-1] + (-1, 32))
    amax = np.abs(blocks).max(-1, keepdims=True)
    byte = np.maximum(np.where(amax > 0, np.frexp(amax)[1] - 1 + 127, 0) - down, 1)
    scale = np.exp2(byte - 127.0)
    codes = (blocks / scale).astype(np.float32).astype(dtype).astype(np.float64)
    return np.moveaxis((codes * scale).reshape(v.shape), -1, axis)


WIDE = False


def mx_kscale(k):
    if not WIDE:
        return np.ones(k)
    levels = np.array([10, -10, 5, -5, 0])
    if k % 512:
        return np.exp2(np.random.permutation(np.resize(levels, k // 32))).repeat(32)
    a = np.empty((k // 512, 16))
    for p in range(k // 512):
        a[p, :8] = np.random.permutation(np.resize(levels, 8))
        for g in range(8):
            far = levels[np.abs(levels - a[p, g]) >= 10]
            a[p, g + 8] = far[np.random.randint(len(far))]
    return np.exp2(a.ravel()).repeat(32)


def f64(x):
    return np.asarray(x).astype(np.float64)


def striped8(idx):
    return np.asarray(idx).reshape(8, -1, 16).transpose(0, 2, 1).reshape(128, -1).astype(np.uint16)


def unstriped8(offs):
    return offs.reshape(8, 16, -1).transpose(0, 2, 1).reshape(8, -1).astype(np.int64)


def pick8(x, idx, run):
    r = np.arange(len(x))
    return x[r[:, None], idx[r % (8 * run) // run]]


E2M1 = np.array([0.0, 0.5, 1.0, 1.5, 2.0, 3.0, 4.0, 6.0, -0.0, -0.5, -1.0, -1.5, -2.0, -3.0, -4.0, -6.0])


def pack_weight(w, fmt):
    k, n = w.shape
    w = f64(np.asarray(w, np.float32).astype(ml_dtypes.bfloat16)).reshape(k // 32, 32, n)
    amax = np.abs(w).max(1)
    if fmt == "e4m3":
        byte = np.frexp(amax)[1] - 1 + 127 - 7
    else:
        mant, ex = np.frexp(amax / 6.0)
        byte = np.where(mant > 0.5, ex, ex - 1) + 127
    byte = np.clip(np.where(amax > 0, byte, 1), 1, 254)
    scaled = (w * np.exp2(127.0 - byte)[:, None, :]).reshape(k, n).astype(np.float32)
    by_word = np.ascontiguousarray(scaled.reshape(k // 512, 128, 4, n).transpose(0, 1, 3, 2))
    if fmt == "e4m3":
        words = by_word.astype(ml_dtypes.float8_e4m3fn).view(np.uint8)
    else:
        c = by_word.astype(ml_dtypes.float4_e2m1fn).view(np.uint8) & 0xF
        words = (c[..., 0::2] | (c[..., 1::2] << 4)).reshape(k // 512, 128, 2 * n)
    return np.ascontiguousarray(words), np.ascontiguousarray(byte.astype(np.uint8).reshape(k // 512, 16, n))


def unpack_weight(words, scales, fmt):
    g, _, n = scales.shape
    words = np.ascontiguousarray(words).reshape(g, 128, n, -1)
    if fmt == "e4m3":
        vals = words.view(ml_dtypes.float8_e4m3fn).astype(np.float64)
    else:
        nib = np.empty((g, 128, n, 4), np.uint8)
        nib[..., 0::2] = words & 0xF
        nib[..., 1::2] = words >> 4
        vals = E2M1[nib]
    vals = vals * np.repeat(np.exp2(scales.astype(np.float64) - 127.0), 8, axis=1)[..., None]
    return vals.transpose(0, 1, 3, 2).reshape(g * 512, n)


D, E, T, Q, I = 512, 512, 1024, 128, 256


def setup_inputs():
    n = np.random.standard_normal
    idx = np.stack([np.random.permutation(T)[:I] for _ in range(8)])
    fd = mx_kscale(D)
    fe = mx_kscale(E)
    keysp = pack_weight(n((D, T)) / fd[:, None], "e2m1")
    return {
        "query": (n((D, Q)) * 0.6 / np.sqrt(D) * fd[:, None]).astype(np.float32),
        "keys_words": keysp[0],
        "keys_scales": keysp[1],
        "gout": (n((E, Q)) * 1 / np.sqrt(E) * fe[:, None]).astype(np.float32),
        "vals": (n((E, T)) / fe[:, None]).astype(np.float32),
        "zp": (np.random.uniform(200.0, 800.0, (Q, 1))).astype(np.float32),
        "cp": (np.random.uniform(-100.0, 100.0, (Q, 1))).astype(np.float32),
        "old": (0.5 * n((Q, T))).astype(np.float32),
        "offs": striped8(idx),
    }


def reference(query, keys_words, keys_scales, gout, vals, zp, cp, old, offs):
    idx = unstriped8(offs)
    keysu = unpack_weight(keys_words, keys_scales, "e2m1")
    queryq = mxq(f64(query), 0, "e4m3")
    a = queryq.T @ keysu
    p = np.exp(pick8(a, idx, 16))
    z = np.sum(p, axis=1, keepdims=True) + f64(zp)
    goutq = mxq(f64(gout), 0, "e4m3")
    valsq = mxq(f64(vals), 0, "e4m3")
    c0 = goutq.T @ valsq
    dz = (np.sum(p * pick8(c0, idx, 16), axis=1, keepdims=True) + f64(cp)) / np.square(z) * (-1.0)
    dp = 1.0 / z * pick8(c0, idx, 16) + dz
    e1 = dp * p
    s1 = np.zeros((Q, T))
    s1[np.arange(Q)[:, None], idx[np.arange(Q) % 128 // 16]] = e1
    y = s1 * 1024.0 + f64(old)
    return y

@@ -1,0 +1,180 @@
+from contextlib import ExitStack
+
+import concourse.mybir as mybir
+
+D, E, T, Q, SLOTS = 512, 512, 1024, 128, 256
+FLOPS = 2 * (D + E) * Q * T
+
+F32 = mybir.dt.float32
+BF16 = mybir.dt.bfloat16
+I32 = mybir.dt.int32
+U32 = mybir.dt.uint32
+U16 = mybir.dt.uint16
+U8 = mybir.dt.uint8
+FP8X4 = mybir.dt.float8_e4m3fn_x4
+FP4X4 = mybir.dt.float4_e2m1fn_x4
+ALU = mybir.AluOpType
+ACT = mybir.ActivationFunctionType
+
+P = 128
+PACK = 4
+BANK = 512
+VALS_CHUNKS = (256, 256, 256, 128, 128)
+STORE_COLS = 256
+
+
+def interleave(copy, grouped, raw, lo, hi):
+    copy(
+        out=grouped[:, lo:hi, :].rearrange("p (c i) t -> p c t i", i=PACK),
+        in_=raw[:, :, lo:hi].rearrange("p t (c i) -> p c t i", i=PACK),
+    )
+
+
+def quantize(nc, pool, name, grouped, width):
+    codes = pool.tile([P, width], U32, name=name + "_codes", align_bytes=64)
+    scales = pool.tile([P, width], U8, name=name + "_scales", align_bytes=64)
+    nc.vector.quantize_mx(
+        out=codes[:].bitcast(FP8X4), scales=scales[:], in_=grouped[:].rearrange("p w t -> p (w t)")
+    )
+    return codes, scales
+
+
+def tile_attend_bsharedprefix_heads_kernel(
+    tc, query, keys_words, keys_scales, gout, vals, zp, cp, old, offs, out
+):
+    nc = tc.nc
+    with ExitStack() as ctx:
+        sb = ctx.enter_context(tc.tile_pool(name="sb", bufs=1))
+        psum = ctx.enter_context(tc.psum_pool(name="psum", bufs=1))
+
+        key_scales = sb.tile([P, T], U8, align_bytes=64)
+        nc.gpsimd.memset(key_scales[:].bitcast(I32), 0)
+        for quad in range(4):
+            nc.scalar.dma_start(
+                out=key_scales[32 * quad : 32 * quad + 4, :].bitcast(I32),
+                in_=keys_scales[0, 4 * quad : 4 * quad + 4, :].bitcast(I32),
+            )
+        zp_col = sb.tile([P, 1], F32)
+        cp_col = sb.tile([P, 1], F32)
+        nc.gpsimd.dma_start(out=zp_col[:], in_=zp)
+        nc.gpsimd.dma_start(out=cp_col[:], in_=cp)
+        placed = sb.tile([P, T], F32)
+        nc.gpsimd.memset(placed[:], 0.0)
+
+        def scalar_copy(out, in_):
+            nc.scalar.activation(out=out, in_=in_, func=ACT.Copy)
+
+        offsets = sb.tile([P, SLOTS // 16], U16)
+        nc.sync.dma_start(offsets[:], offs)
+        query_raw = sb.tile([P, PACK, Q], F32)
+        nc.sync.dma_start(out=query_raw[:], in_=query.rearrange("(p t) q -> p t q", t=PACK))
+        key_words = sb.tile([P, 2 * T], U8, align_bytes=64)
+        nc.sync.dma_start(out=key_words[:].bitcast(I32), in_=keys_words[0].bitcast(I32))
+        gout_raw = sb.tile([P, PACK, Q], F32)
+        nc.sync.dma_start(out=gout_raw[:], in_=gout.rearrange("(p t) q -> p t q", t=PACK))
+        vals_rows = vals.rearrange("(p t) w -> p t w", t=PACK)
+        vals_raw = []
+        start = 0
+        for n, width in enumerate(VALS_CHUNKS):
+            raw = sb.tile([P, PACK, width], F32, name="vals_raw%d" % n)
+            nc.sync.dma_start(out=raw[:], in_=vals_rows[:, :, start : start + width])
+            vals_raw.append((start, width, raw))
+            start = start + width
+        old_sb = sb.tile([P, T], F32)
+        nc.sync.dma_start(out=old_sb[:], in_=old)
+
+        query_grouped = sb.tile([P, Q, PACK], BF16, align_bytes=64)
+        interleave(nc.vector.tensor_copy, query_grouped, query_raw, 0, Q)
+        query_codes, query_scales = quantize(nc, sb, "query", query_grouped, Q)
+        gout_grouped = sb.tile([P, Q, PACK], BF16, align_bytes=64)
+        interleave(nc.vector.tensor_copy, gout_grouped, gout_raw, 0, Q)
+        gout_codes, gout_scales = quantize(nc, sb, "gout", gout_grouped, Q)
+
+        scores = sb.tile([P, T], F32)
+        for b in range(T // BANK):
+            bank = psum.tile([P, BANK], F32, name="score_bank%d" % b)
+            nc.tensor.matmul_mx(
+                out=bank[:],
+                lhsT=query_codes[:].bitcast(FP8X4),
+                lhsT_scale=query_scales[:],
+                rhs=key_words[:, 2 * BANK * b : 2 * BANK * (b + 1)].bitcast(FP4X4),
+                rhs_scale=key_scales[:, BANK * b : BANK * (b + 1)],
+                start=True,
+                stop=True,
+            )
+            scalar_copy(out=scores[:, BANK * b : BANK * (b + 1)], in_=bank[:])
+
+        listed_scores = sb.tile([P, SLOTS], F32)
+        nc.vector.tensor_copy(listed_scores[:], scores[:].indirect(offsets[:]))
+        negated = sb.tile([P, SLOTS], F32)
+        neg_shift = sb.tile([P, 1], F32)
+        nc.vector.tensor_scalar(
+            out=negated[:], in0=listed_scores[:], scalar1=-1.0, scalar2=0.0,
+            op0=ALU.mult, op1=ALU.min, accum_out=neg_shift[:],
+        )
+        expo = sb.tile([P, SLOTS], F32)
+        expo_sum = sb.tile([P, 1], F32)
+        shrink = sb.tile([P, 1], F32)
+        nc.scalar.activation(
+            out=expo[:], in_=listed_scores[:], func=ACT.Exp, bias=neg_shift[:], accum_out=expo_sum[:]
+        )
+        nc.scalar.activation(out=shrink[:], in_=neg_shift[:], func=ACT.Exp)
+        norm = sb.tile([P, 1], F32)
+        nc.vector.tensor_scalar(
+            out=norm[:], in0=zp_col[:], scalar1=shrink[:], scalar2=expo_sum[:], op0=ALU.mult, op1=ALU.add
+        )
+        inv_norm = sb.tile([P, 1], F32)
+        nc.vector.reciprocal(out=inv_norm[:], in_=norm[:])
+        prob = sb.tile([P, SLOTS], F32)
+        nc.vector.tensor_scalar(
+            out=prob[:], in0=expo[:], scalar1=inv_norm[:], scalar2=None, op0=ALU.mult
+        )
+        prefix_mean = sb.tile([P, 1], F32)
+        nc.vector.tensor_scalar(
+            out=prefix_mean[:], in0=cp_col[:], scalar1=shrink[:], scalar2=inv_norm[:],
+            op0=ALU.mult, op1=ALU.mult,
+        )
+
+        prods = sb.tile([P, T], F32)
+        for n, (start, width, raw) in enumerate(vals_raw):
+            grouped = sb.tile([P, width, PACK], BF16, name="vals_grouped%d" % n, align_bytes=64)
+            split = width * 5 // 8
+            interleave(nc.vector.tensor_copy, grouped, raw, 0, split)
+            interleave(scalar_copy, grouped, raw, split, width)
+            codes, scales = quantize(nc, sb, "vals%d" % n, grouped, width)
+            bank = psum.tile([P, width], F32, name="prod_bank%d" % n)
+            nc.tensor.matmul_mx(
+                out=bank[:],
+                lhsT=gout_codes[:].bitcast(FP8X4),
+                lhsT_scale=gout_scales[:],
+                rhs=codes[:].bitcast(FP8X4),
+                rhs_scale=scales[:],
+                start=True,
+                stop=True,
+            )
+            scalar_copy(out=prods[:, start : start + width], in_=bank[:])
+
+        listed_prods = sb.tile([P, SLOTS], F32)
+        nc.vector.tensor_copy(listed_prods[:], prods[:].indirect(offsets[:]))
+        weighted = sb.tile([P, SLOTS], F32)
+        suffix_mean = sb.tile([P, 1], F32)
+        nc.vector.scalar_tensor_tensor(
+            out=weighted[:], in0=listed_prods[:], scalar=1.0, in1=prob[:],
+            op0=ALU.mult, op1=ALU.mult, accum_out=suffix_mean[:],
+        )
+        centred = sb.tile([P, SLOTS], F32)
+        nc.vector.tensor_scalar(
+            out=centred[:], in0=listed_prods[:], scalar1=suffix_mean[:], scalar2=prefix_mean[:],
+            op0=ALU.subtract, op1=ALU.subtract,
+        )
+        nc.vector.tensor_tensor(placed[:].indirect(offsets[:]), centred[:], prob[:], ALU.mult)
+
+        result = sb.tile([P, T], F32)
+        for n in range(T // STORE_COLS):
+            cols = slice(n * STORE_COLS, (n + 1) * STORE_COLS)
+            nc.vector.scalar_tensor_tensor(
+                out=result[:, cols], in0=placed[:, cols], scalar=1024.0, in1=old_sb[:, cols],
+                op0=ALU.mult, op1=ALU.add,
+            )
+            queue = nc.sync if n % 2 == 0 else nc.scalar
+            queue.dma_start(out=out[:, cols], in_=result[:, cols])

@@ -19,23 +19,27 @@ ACT = mybir.ActivationFunctionType
 P = 128
 PACK = 4
 BANK = 512
-VALS_CHUNKS = (256, 256, 256, 128, 128)
-STORE_COLS = 256
+VALS_CHUNKS = (128, 256, 256, 256, 128)
+VECTOR_COLS = (128, 0, 256, 128, 0)
+STORE_CHUNKS = (256, 256, 256, 256)
 
 
-def interleave(copy, grouped, raw, lo, hi):
+def interleave(copy, grouped, raw):
     copy(
-        out=grouped[:, lo:hi, :].rearrange("p (c i) t -> p c t i", i=PACK),
-        in_=raw[:, :, lo:hi].rearrange("p t (c i) -> p c t i", i=PACK),
+        out=grouped.rearrange("p (c i) t -> p c t i", i=PACK),
+        in_=raw.rearrange("p t (c i) -> p c t i", i=PACK),
     )
 
 
-def quantize(nc, pool, name, grouped, width):
+def quantize(nc, pool, name, grouped, width, piece):
     codes = pool.tile([P, width], U32, name=name + "_codes", align_bytes=64)
     scales = pool.tile([P, width], U8, name=name + "_scales", align_bytes=64)
-    nc.vector.quantize_mx(
-        out=codes[:].bitcast(FP8X4), scales=scales[:], in_=grouped[:].rearrange("p w t -> p (w t)")
-    )
+    for lo in range(0, width, piece):
+        nc.vector.quantize_mx(
+            out=codes[:, lo : lo + piece].bitcast(FP8X4),
+            scales=scales[:, lo : lo + piece],
+            in_=grouped[:, lo : lo + piece, :].rearrange("p w t -> p (w t)"),
+        )
     return codes, scales
 
 
@@ -47,48 +51,46 @@ def tile_attend_bsharedprefix_heads_kernel(
         sb = ctx.enter_context(tc.tile_pool(name="sb", bufs=1))
         psum = ctx.enter_context(tc.psum_pool(name="psum", bufs=1))
 
-        key_scales = sb.tile([P, T], U8, align_bytes=64)
-        nc.gpsimd.memset(key_scales[:].bitcast(I32), 0)
-        for quad in range(4):
-            nc.scalar.dma_start(
-                out=key_scales[32 * quad : 32 * quad + 4, :].bitcast(I32),
-                in_=keys_scales[0, 4 * quad : 4 * quad + 4, :].bitcast(I32),
-            )
-        zp_col = sb.tile([P, 1], F32)
-        cp_col = sb.tile([P, 1], F32)
-        nc.gpsimd.dma_start(out=zp_col[:], in_=zp)
-        nc.gpsimd.dma_start(out=cp_col[:], in_=cp)
-        placed = sb.tile([P, T], F32)
-        nc.gpsimd.memset(placed[:], 0.0)
-
         def scalar_copy(out, in_):
             nc.scalar.activation(out=out, in_=in_, func=ACT.Copy)
 
-        offsets = sb.tile([P, SLOTS // 16], U16)
-        nc.sync.dma_start(offsets[:], offs)
+        placed = sb.tile([P, T], F32)
+        nc.gpsimd.memset(placed[:], 0.0)
+
+        vals_rows = vals.rearrange("(p t) w -> p t w", t=PACK)
+        starts = [sum(VALS_CHUNKS[:n]) for n in range(len(VALS_CHUNKS))]
+
+        def load_vals(n):
+            raw = sb.tile([P, PACK, VALS_CHUNKS[n]], F32, name="vals_raw%d" % n, tag="raw%d" % n)
+            nc.sync.dma_start(out=raw[:], in_=vals_rows[:, :, starts[n] : starts[n] + VALS_CHUNKS[n]])
+            return raw
+
         query_raw = sb.tile([P, PACK, Q], F32)
         nc.sync.dma_start(out=query_raw[:], in_=query.rearrange("(p t) q -> p t q", t=PACK))
+        key_scales = sb.tile([P, T], U8, align_bytes=64)
+        for quad in range(4):
+            nc.sync.dma_start(
+                out=key_scales[32 * quad : 32 * quad + 4, :].bitcast(I32),
+                in_=keys_scales[0, 4 * quad : 4 * quad + 4, :].bitcast(I32),
+            )
         key_words = sb.tile([P, 2 * T], U8, align_bytes=64)
         nc.sync.dma_start(out=key_words[:].bitcast(I32), in_=keys_words[0].bitcast(I32))
         gout_raw = sb.tile([P, PACK, Q], F32)
         nc.sync.dma_start(out=gout_raw[:], in_=gout.rearrange("(p t) q -> p t q", t=PACK))
-        vals_rows = vals.rearrange("(p t) w -> p t w", t=PACK)
-        vals_raw = []
-        start = 0
-        for n, width in enumerate(VALS_CHUNKS):
-            raw = sb.tile([P, PACK, width], F32, name="vals_raw%d" % n)
-            nc.sync.dma_start(out=raw[:], in_=vals_rows[:, :, start : start + width])
-            vals_raw.append((start, width, raw))
-            start = start + width
+        vals_raw = [load_vals(0), load_vals(1)]
+        offsets = sb.tile([P, SLOTS // 16], U16)
+        nc.sync.dma_start(offsets[:], offs)
+        vals_raw.extend(load_vals(n) for n in range(2, len(VALS_CHUNKS)))
+        zp_col = sb.tile([P, 1], F32)
+        nc.sync.dma_start(out=zp_col[:], in_=zp)
+        cp_col = sb.tile([P, 1], F32)
+        nc.sync.dma_start(out=cp_col[:], in_=cp)
         old_sb = sb.tile([P, T], F32)
         nc.sync.dma_start(out=old_sb[:], in_=old)
 
         query_grouped = sb.tile([P, Q, PACK], BF16, align_bytes=64)
-        interleave(nc.vector.tensor_copy, query_grouped, query_raw, 0, Q)
-        query_codes, query_scales = quantize(nc, sb, "query", query_grouped, Q)
-        gout_grouped = sb.tile([P, Q, PACK], BF16, align_bytes=64)
-        interleave(nc.vector.tensor_copy, gout_grouped, gout_raw, 0, Q)
-        gout_codes, gout_scales = quantize(nc, sb, "gout", gout_grouped, Q)
+        interleave(nc.vector.tensor_copy, query_grouped[:], query_raw[:])
+        query_codes, query_scales = quantize(nc, sb, "query", query_grouped, Q, Q)
 
         scores = sb.tile([P, T], F32)
         for b in range(T // BANK):
@@ -104,7 +106,12 @@ def tile_attend_bsharedprefix_heads_kernel(
             )
             scalar_copy(out=scores[:, BANK * b : BANK * (b + 1)], in_=bank[:])
 
-        listed_scores = sb.tile([P, SLOTS], F32)
+        first_grouped = sb.tile([P, 2 * Q, PACK], BF16, tag="first", align_bytes=64)
+        interleave(nc.vector.tensor_copy, first_grouped[:, :Q, :], gout_raw[:])
+        interleave(nc.vector.tensor_copy, first_grouped[:, Q:, :], vals_raw[0][:])
+        first_codes, first_scales = quantize(nc, sb, "first", first_grouped, 2 * Q, 2 * Q)
+
+        listed_scores = sb.tile([P, SLOTS], F32, tag="first", align_bytes=64)
         nc.vector.tensor_copy(listed_scores[:], scores[:].indirect(offsets[:]))
         negated = sb.tile([P, SLOTS], F32)
         neg_shift = sb.tile([P, 1], F32)
@@ -119,43 +126,51 @@ def tile_attend_bsharedprefix_heads_kernel(
             out=expo[:], in_=listed_scores[:], func=ACT.Exp, bias=neg_shift[:], accum_out=expo_sum[:]
         )
         nc.scalar.activation(out=shrink[:], in_=neg_shift[:], func=ACT.Exp)
+
+        def multiply(n, codes, scales):
+            bank = psum.tile([P, VALS_CHUNKS[n]], F32, name="prod_bank%d" % n)
+            nc.tensor.matmul_mx(
+                out=bank[:],
+                lhsT=first_codes[:, :Q].bitcast(FP8X4),
+                lhsT_scale=first_scales[:, :Q],
+                rhs=codes.bitcast(FP8X4),
+                rhs_scale=scales,
+                start=True,
+                stop=True,
+            )
+            return bank
+
+        banks = [multiply(0, first_codes[:, Q:], first_scales[:, Q:])]
+        for n in range(1, len(VALS_CHUNKS)):
+            width = VALS_CHUNKS[n]
+            grouped = sb.tile([P, width, PACK], BF16, name="vals_grouped%d" % n, align_bytes=64)
+            for lo in range(0, VECTOR_COLS[n], Q):
+                interleave(nc.vector.tensor_copy, grouped[:, lo : lo + Q, :], vals_raw[n][:, :, lo : lo + Q])
+            if VECTOR_COLS[n] < width:
+                interleave(scalar_copy, grouped[:, VECTOR_COLS[n] :, :], vals_raw[n][:, :, VECTOR_COLS[n] :])
+            piece = Q if VECTOR_COLS[n] == width else width
+            codes, scales = quantize(nc, sb, "vals%d" % n, grouped, width, piece)
+            banks.append(multiply(n, codes[:], scales[:]))
+
+        prods = sb.tile([P, T], F32, tag="raw%d" % (len(VALS_CHUNKS) - 1))
+        for n, width in enumerate(VALS_CHUNKS):
+            scalar_copy(out=prods[:, starts[n] : starts[n] + width], in_=banks[n][:])
+
         norm = sb.tile([P, 1], F32)
         nc.vector.tensor_scalar(
             out=norm[:], in0=zp_col[:], scalar1=shrink[:], scalar2=expo_sum[:], op0=ALU.mult, op1=ALU.add
         )
         inv_norm = sb.tile([P, 1], F32)
         nc.vector.reciprocal(out=inv_norm[:], in_=norm[:])
+        listed_prods = sb.tile([P, SLOTS], F32)
+        nc.vector.tensor_copy(listed_prods[:], prods[:].indirect(offsets[:]))
         prob = sb.tile([P, SLOTS], F32)
-        nc.vector.tensor_scalar(
-            out=prob[:], in0=expo[:], scalar1=inv_norm[:], scalar2=None, op0=ALU.mult
-        )
+        nc.scalar.activation(out=prob[:], in_=expo[:], func=ACT.Copy, scale=inv_norm[:])
         prefix_mean = sb.tile([P, 1], F32)
         nc.vector.tensor_scalar(
             out=prefix_mean[:], in0=cp_col[:], scalar1=shrink[:], scalar2=inv_norm[:],
             op0=ALU.mult, op1=ALU.mult,
         )
-
-        prods = sb.tile([P, T], F32)
-        for n, (start, width, raw) in enumerate(vals_raw):
-            grouped = sb.tile([P, width, PACK], BF16, name="vals_grouped%d" % n, align_bytes=64)
-            split = width * 5 // 8
-            interleave(nc.vector.tensor_copy, grouped, raw, 0, split)
-            interleave(scalar_copy, grouped, raw, split, width)
-            codes, scales = quantize(nc, sb, "vals%d" % n, grouped, width)
-            bank = psum.tile([P, width], F32, name="prod_bank%d" % n)
-            nc.tensor.matmul_mx(
-                out=bank[:],
-                lhsT=gout_codes[:].bitcast(FP8X4),
-                lhsT_scale=gout_scales[:],
-                rhs=codes[:].bitcast(FP8X4),
-                rhs_scale=scales[:],
-                start=True,
-                stop=True,
-            )
-            scalar_copy(out=prods[:, start : start + width], in_=bank[:])
-
-        listed_prods = sb.tile([P, SLOTS], F32)
-        nc.vector.tensor_copy(listed_prods[:], prods[:].indirect(offsets[:]))
         weighted = sb.tile([P, SLOTS], F32)
         suffix_mean = sb.tile([P, 1], F32)
         nc.vector.scalar_tensor_tensor(
@@ -170,8 +185,8 @@ def tile_attend_bsharedprefix_heads_kernel(
         nc.vector.tensor_tensor(placed[:].indirect(offsets[:]), centred[:], prob[:], ALU.mult)
 
         result = sb.tile([P, T], F32)
-        for n in range(T // STORE_COLS):
-            cols = slice(n * STORE_COLS, (n + 1) * STORE_COLS)
+        for n, width in enumerate(STORE_CHUNKS):
+            cols = slice(sum(STORE_CHUNKS[:n]), sum(STORE_CHUNKS[:n]) + width)
             nc.vector.scalar_tensor_tensor(
                 out=result[:, cols], in0=placed[:, cols], scalar=1024.0, in1=old_sb[:, cols],
                 op0=ALU.mult, op1=ALU.add,

@@ -19,8 +19,9 @@ ACT = mybir.ActivationFunctionType
 P = 128
 PACK = 4
 BANK = 512
-VALS_CHUNKS = (128, 256, 256, 256, 128)
-VECTOR_COLS = (128, 0, 256, 128, 0)
+VALS_CHUNKS = (128, 512, 256, 128)
+PIECES = ((1, 0, 256, 256), (1, 256, 256, 128), (2, 0, 256, 128), (3, 0, 128, 0))
+SCORE_COLS = 256
 STORE_CHUNKS = (256, 256, 256, 256)
 
 
@@ -68,19 +69,18 @@ def tile_attend_bsharedprefix_heads_kernel(
         query_raw = sb.tile([P, PACK, Q], F32)
         nc.sync.dma_start(out=query_raw[:], in_=query.rearrange("(p t) q -> p t q", t=PACK))
         key_scales = sb.tile([P, T], U8, align_bytes=64)
-        for quad in range(4):
+        for r in range(4):
             nc.sync.dma_start(
-                out=key_scales[32 * quad : 32 * quad + 4, :].bitcast(I32),
-                in_=keys_scales[0, 4 * quad : 4 * quad + 4, :].bitcast(I32),
+                out=key_scales[r:P:32, :].bitcast(I32), in_=keys_scales[0, r:16:4, :].bitcast(I32)
             )
         key_words = sb.tile([P, 2 * T], U8, align_bytes=64)
         nc.sync.dma_start(out=key_words[:].bitcast(I32), in_=keys_words[0].bitcast(I32))
         gout_raw = sb.tile([P, PACK, Q], F32)
         nc.sync.dma_start(out=gout_raw[:], in_=gout.rearrange("(p t) q -> p t q", t=PACK))
-        vals_raw = [load_vals(0), load_vals(1)]
+        vals_raw = [load_vals(0)]
         offsets = sb.tile([P, SLOTS // 16], U16)
         nc.sync.dma_start(offsets[:], offs)
-        vals_raw.extend(load_vals(n) for n in range(2, len(VALS_CHUNKS)))
+        vals_raw.extend(load_vals(n) for n in range(1, len(VALS_CHUNKS)))
         zp_col = sb.tile([P, 1], F32)
         nc.sync.dma_start(out=zp_col[:], in_=zp)
         cp_col = sb.tile([P, 1], F32)
@@ -93,18 +93,18 @@ def tile_attend_bsharedprefix_heads_kernel(
         query_codes, query_scales = quantize(nc, sb, "query", query_grouped, Q, Q)
 
         scores = sb.tile([P, T], F32)
-        for b in range(T // BANK):
-            bank = psum.tile([P, BANK], F32, name="score_bank%d" % b)
+        for b in range(T // SCORE_COLS):
+            bank = psum.tile([P, SCORE_COLS], F32, name="score_bank%d" % b, tag="bank%d" % b)
             nc.tensor.matmul_mx(
                 out=bank[:],
                 lhsT=query_codes[:].bitcast(FP8X4),
                 lhsT_scale=query_scales[:],
-                rhs=key_words[:, 2 * BANK * b : 2 * BANK * (b + 1)].bitcast(FP4X4),
-                rhs_scale=key_scales[:, BANK * b : BANK * (b + 1)],
+                rhs=key_words[:, 2 * SCORE_COLS * b : 2 * SCORE_COLS * (b + 1)].bitcast(FP4X4),
+                rhs_scale=key_scales[:, SCORE_COLS * b : SCORE_COLS * (b + 1)],
                 start=True,
                 stop=True,
             )
-            scalar_copy(out=scores[:, BANK * b : BANK * (b + 1)], in_=bank[:])
+            scalar_copy(out=scores[:, SCORE_COLS * b : SCORE_COLS * (b + 1)], in_=bank[:])
 
         first_grouped = sb.tile([P, 2 * Q, PACK], BF16, tag="first", align_bytes=64)
         interleave(nc.vector.tensor_copy, first_grouped[:, :Q, :], gout_raw[:])
@@ -127,8 +127,8 @@ def tile_attend_bsharedprefix_heads_kernel(
         )
         nc.scalar.activation(out=shrink[:], in_=neg_shift[:], func=ACT.Exp)
 
-        def multiply(n, codes, scales):
-            bank = psum.tile([P, VALS_CHUNKS[n]], F32, name="prod_bank%d" % n)
+        def multiply(n, width, codes, scales):
+            bank = psum.tile([P, width], F32, name="prod_bank%d" % n, tag="bank%d" % ((n + 4) % 8))
             nc.tensor.matmul_mx(
                 out=bank[:],
                 lhsT=first_codes[:, :Q].bitcast(FP8X4),
@@ -140,21 +140,24 @@ def tile_attend_bsharedprefix_heads_kernel(
             )
             return bank
 
-        banks = [multiply(0, first_codes[:, Q:], first_scales[:, Q:])]
-        for n in range(1, len(VALS_CHUNKS)):
-            width = VALS_CHUNKS[n]
+        banks = [(0, Q, multiply(0, Q, first_codes[:, Q:], first_scales[:, Q:]))]
+        staged = []
+        for n, (chunk, lo, width, vector_cols) in enumerate(PIECES):
             grouped = sb.tile([P, width, PACK], BF16, name="vals_grouped%d" % n, align_bytes=64)
-            for lo in range(0, VECTOR_COLS[n], Q):
-                interleave(nc.vector.tensor_copy, grouped[:, lo : lo + Q, :], vals_raw[n][:, :, lo : lo + Q])
-            if VECTOR_COLS[n] < width:
-                interleave(scalar_copy, grouped[:, VECTOR_COLS[n] :, :], vals_raw[n][:, :, VECTOR_COLS[n] :])
-            piece = Q if VECTOR_COLS[n] == width else width
-            codes, scales = quantize(nc, sb, "vals%d" % n, grouped, width, piece)
-            banks.append(multiply(n, codes[:], scales[:]))
+            raw = vals_raw[chunk][:, :, lo : lo + width]
+            if vector_cols > 0:
+                interleave(nc.vector.tensor_copy, grouped[:, :vector_cols, :], raw[:, :, :vector_cols])
+            if vector_cols < width:
+                interleave(scalar_copy, grouped[:, vector_cols:, :], raw[:, :, vector_cols:])
+            staged.append(grouped)
+        for n, (chunk, lo, width, vector_cols) in enumerate(PIECES):
+            codes, scales = quantize(nc, sb, "vals%d" % n, staged[n], width, width)
+            banks.append((starts[chunk] + lo, width, multiply(n + 1, width, codes[:], scales[:])))
 
         prods = sb.tile([P, T], F32, tag="raw%d" % (len(VALS_CHUNKS) - 1))
-        for n, width in enumerate(VALS_CHUNKS):
-            scalar_copy(out=prods[:, starts[n] : starts[n] + width], in_=banks[n][:])
+        for n, (start, width, bank) in enumerate(banks):
+            copy = nc.vector.tensor_copy if n == len(banks) - 2 else scalar_copy
+            copy(out=prods[:, start : start + width], in_=bank[:])
 
         norm = sb.tile([P, 1], F32)
         nc.vector.tensor_scalar(
@@ -191,5 +194,4 @@ def tile_attend_bsharedprefix_heads_kernel(
                 out=result[:, cols], in0=placed[:, cols], scalar=1024.0, in1=old_sb[:, cols],
                 op0=ALU.mult, op1=ALU.add,
             )
-            queue = nc.sync if n % 2 == 0 else nc.scalar
-            queue.dma_start(out=out[:, cols], in_=result[:, cols])
+            nc.sync.dma_start(out=out[:, cols], in_=result[:, cols])

@@ -19,8 +19,9 @@ ACT = mybir.ActivationFunctionType
 P = 128
 PACK = 4
 BANK = 512
-VALS_CHUNKS = (128, 512, 256, 128)
-PIECES = ((1, 0, 256, 256), (1, 256, 256, 128), (2, 0, 256, 128), (3, 0, 128, 0))
+VALS_CHUNKS = (256, 384, 256, 128)
+VECTOR_COLS = (0, 256, 128, 0)
+QUANT_COLS = (256, 128, 256, 128)
 SCORE_COLS = 256
 STORE_CHUNKS = (256, 256, 256, 256)
 
@@ -106,12 +107,11 @@ def tile_attend_bsharedprefix_heads_kernel(
             )
             scalar_copy(out=scores[:, SCORE_COLS * b : SCORE_COLS * (b + 1)], in_=bank[:])
 
-        first_grouped = sb.tile([P, 2 * Q, PACK], BF16, tag="first", align_bytes=64)
-        interleave(nc.vector.tensor_copy, first_grouped[:, :Q, :], gout_raw[:])
-        interleave(nc.vector.tensor_copy, first_grouped[:, Q:, :], vals_raw[0][:])
-        first_codes, first_scales = quantize(nc, sb, "first", first_grouped, 2 * Q, 2 * Q)
+        gout_grouped = sb.tile([P, Q, PACK], BF16, align_bytes=64)
+        interleave(nc.vector.tensor_copy, gout_grouped[:], gout_raw[:])
+        gout_codes, gout_scales = quantize(nc, sb, "gout", gout_grouped, Q, Q)
 
-        listed_scores = sb.tile([P, SLOTS], F32, tag="first", align_bytes=64)
+        listed_scores = sb.tile([P, SLOTS], F32)
         nc.vector.tensor_copy(listed_scores[:], scores[:].indirect(offsets[:]))
         negated = sb.tile([P, SLOTS], F32)
         neg_shift = sb.tile([P, 1], F32)
@@ -127,37 +127,32 @@ def tile_attend_bsharedprefix_heads_kernel(
         )
         nc.scalar.activation(out=shrink[:], in_=neg_shift[:], func=ACT.Exp)
 
-        def multiply(n, width, codes, scales):
-            bank = psum.tile([P, width], F32, name="prod_bank%d" % n, tag="bank%d" % ((n + 4) % 8))
-            nc.tensor.matmul_mx(
-                out=bank[:],
-                lhsT=first_codes[:, :Q].bitcast(FP8X4),
-                lhsT_scale=first_scales[:, :Q],
-                rhs=codes.bitcast(FP8X4),
-                rhs_scale=scales,
-                start=True,
-                stop=True,
-            )
-            return bank
-
-        banks = [(0, Q, multiply(0, Q, first_codes[:, Q:], first_scales[:, Q:]))]
-        staged = []
-        for n, (chunk, lo, width, vector_cols) in enumerate(PIECES):
+        banks = []
+        for n, width in enumerate(VALS_CHUNKS):
             grouped = sb.tile([P, width, PACK], BF16, name="vals_grouped%d" % n, align_bytes=64)
-            raw = vals_raw[chunk][:, :, lo : lo + width]
-            if vector_cols > 0:
-                interleave(nc.vector.tensor_copy, grouped[:, :vector_cols, :], raw[:, :, :vector_cols])
-            if vector_cols < width:
-                interleave(scalar_copy, grouped[:, vector_cols:, :], raw[:, :, vector_cols:])
-            staged.append(grouped)
-        for n, (chunk, lo, width, vector_cols) in enumerate(PIECES):
-            codes, scales = quantize(nc, sb, "vals%d" % n, staged[n], width, width)
-            banks.append((starts[chunk] + lo, width, multiply(n + 1, width, codes[:], scales[:])))
+            raw = vals_raw[n]
+            for lo in range(0, VECTOR_COLS[n], Q):
+                interleave(nc.vector.tensor_copy, grouped[:, lo : lo + Q, :], raw[:, :, lo : lo + Q])
+            interleave(scalar_copy, grouped[:, VECTOR_COLS[n] :, :], raw[:, :, VECTOR_COLS[n] :])
+            codes, scales = quantize(nc, sb, "vals%d" % n, grouped, width, QUANT_COLS[n])
+            bank = psum.tile([P, width], F32, name="prod_bank%d" % n)
+            for lo in range(0, width, 256):
+                cols = slice(lo, min(lo + 256, width))
+                nc.tensor.matmul_mx(
+                    out=bank[:, cols],
+                    lhsT=gout_codes[:].bitcast(FP8X4),
+                    lhsT_scale=gout_scales[:],
+                    rhs=codes[:, cols].bitcast(FP8X4),
+                    rhs_scale=scales[:, cols],
+                    start=True,
+                    stop=True,
+                )
+            banks.append(bank)
 
         prods = sb.tile([P, T], F32, tag="raw%d" % (len(VALS_CHUNKS) - 1))
-        for n, (start, width, bank) in enumerate(banks):
+        for n, width in enumerate(VALS_CHUNKS):
             copy = nc.vector.tensor_copy if n == len(banks) - 2 else scalar_copy
-            copy(out=prods[:, start : start + width], in_=bank[:])
+            copy(out=prods[:, starts[n] : starts[n] + width], in_=banks[n][:])
 
         norm = sb.tile([P, 1], F32)
         nc.vector.tensor_scalar(
@@ -177,7 +172,7 @@ def tile_attend_bsharedprefix_heads_kernel(
         weighted = sb.tile([P, SLOTS], F32)
         suffix_mean = sb.tile([P, 1], F32)
         nc.vector.scalar_tensor_tensor(
-            out=weighted[:], in0=listed_prods[:], scalar=1.0, in1=prob[:],
+            out=weighted[:], in0=listed_prods[:], scalar=inv_norm[:], in1=expo[:],
             op0=ALU.mult, op1=ALU.mult, accum_out=suffix_mean[:],
         )
         centred = sb.tile([P, SLOTS], F32)

from contextlib import ExitStack

import concourse.mybir as mybir

D, E, T, Q, SLOTS = 512, 512, 1024, 128, 256
FLOPS = 2 * (D + E) * Q * T

F32 = mybir.dt.float32
BF16 = mybir.dt.bfloat16
I32 = mybir.dt.int32
U32 = mybir.dt.uint32
U16 = mybir.dt.uint16
U8 = mybir.dt.uint8
FP8X4 = mybir.dt.float8_e4m3fn_x4
FP4X4 = mybir.dt.float4_e2m1fn_x4
ALU = mybir.AluOpType
ACT = mybir.ActivationFunctionType

P = 128
PACK = 4
BANK = 512
VALS_CHUNKS = (256, 384, 256, 128)
VECTOR_COLS = (0, 256, 128, 0)
QUANT_COLS = (256, 128, 256, 128)
SCORE_COLS = 256
STORE_CHUNKS = (256, 256, 256, 256)


def interleave(copy, grouped, raw):
    copy(
        out=grouped.rearrange("p (c i) t -> p c t i", i=PACK),
        in_=raw.rearrange("p t (c i) -> p c t i", i=PACK),
    )


def quantize(nc, pool, name, grouped, width, piece):
    codes = pool.tile([P, width], U32, name=name + "_codes", align_bytes=64)
    scales = pool.tile([P, width], U8, name=name + "_scales", align_bytes=64)
    for lo in range(0, width, piece):
        nc.vector.quantize_mx(
            out=codes[:, lo : lo + piece].bitcast(FP8X4),
            scales=scales[:, lo : lo + piece],
            in_=grouped[:, lo : lo + piece, :].rearrange("p w t -> p (w t)"),
        )
    return codes, scales


def tile_attend_bsharedprefix_heads_kernel(
    tc, query, keys_words, keys_scales, gout, vals, zp, cp, old, offs, out
):
    nc = tc.nc
    with ExitStack() as ctx:
        sb = ctx.enter_context(tc.tile_pool(name="sb", bufs=1))
        psum = ctx.enter_context(tc.psum_pool(name="psum", bufs=1))

        def scalar_copy(out, in_):
            nc.scalar.activation(out=out, in_=in_, func=ACT.Copy)

        placed = sb.tile([P, T], F32)
        nc.gpsimd.memset(placed[:], 0.0)

        vals_rows = vals.rearrange("(p t) w -> p t w", t=PACK)
        starts = [sum(VALS_CHUNKS[:n]) for n in range(len(VALS_CHUNKS))]

        def load_vals(n):
            raw = sb.tile([P, PACK, VALS_CHUNKS[n]], F32, name="vals_raw%d" % n, tag="raw%d" % n)
            nc.sync.dma_start(out=raw[:], in_=vals_rows[:, :, starts[n] : starts[n] + VALS_CHUNKS[n]])
            return raw

        query_raw = sb.tile([P, PACK, Q], F32)
        nc.sync.dma_start(out=query_raw[:], in_=query.rearrange("(p t) q -> p t q", t=PACK))
        key_scales = sb.tile([P, T], U8, align_bytes=64)
        for r in range(4):
            nc.sync.dma_start(
                out=key_scales[r:P:32, :].bitcast(I32), in_=keys_scales[0, r:16:4, :].bitcast(I32)
            )
        key_words = sb.tile([P, 2 * T], U8, align_bytes=64)
        nc.sync.dma_start(out=key_words[:].bitcast(I32), in_=keys_words[0].bitcast(I32))
        gout_raw = sb.tile([P, PACK, Q], F32)
        nc.sync.dma_start(out=gout_raw[:], in_=gout.rearrange("(p t) q -> p t q", t=PACK))
        vals_raw = [load_vals(0)]
        offsets = sb.tile([P, SLOTS // 16], U16)
        nc.sync.dma_start(offsets[:], offs)
        vals_raw.extend(load_vals(n) for n in range(1, len(VALS_CHUNKS)))
        zp_col = sb.tile([P, 1], F32)
        nc.sync.dma_start(out=zp_col[:], in_=zp)
        cp_col = sb.tile([P, 1], F32)
        nc.sync.dma_start(out=cp_col[:], in_=cp)
        old_sb = sb.tile([P, T], F32)
        nc.sync.dma_start(out=old_sb[:], in_=old)

        query_grouped = sb.tile([P, Q, PACK], BF16, align_bytes=64)
        interleave(nc.vector.tensor_copy, query_grouped[:], query_raw[:])
        query_codes, query_scales = quantize(nc, sb, "query", query_grouped, Q, Q)

        scores = sb.tile([P, T], F32)
        for b in range(T // SCORE_COLS):
            bank = psum.tile([P, SCORE_COLS], F32, name="score_bank%d" % b, tag="bank%d" % b)
            nc.tensor.matmul_mx(
                out=bank[:],
                lhsT=query_codes[:].bitcast(FP8X4),
                lhsT_scale=query_scales[:],
                rhs=key_words[:, 2 * SCORE_COLS * b : 2 * SCORE_COLS * (b + 1)].bitcast(FP4X4),
                rhs_scale=key_scales[:, SCORE_COLS * b : SCORE_COLS * (b + 1)],
                start=True,
                stop=True,
            )
            scalar_copy(out=scores[:, SCORE_COLS * b : SCORE_COLS * (b + 1)], in_=bank[:])

        gout_grouped = sb.tile([P, Q, PACK], BF16, align_bytes=64)
        interleave(nc.vector.tensor_copy, gout_grouped[:], gout_raw[:])
        gout_codes, gout_scales = quantize(nc, sb, "gout", gout_grouped, Q, Q)

        listed_scores = sb.tile([P, SLOTS], F32)
        nc.vector.tensor_copy(listed_scores[:], scores[:].indirect(offsets[:]))
        negated = sb.tile([P, SLOTS], F32)
        neg_shift = sb.tile([P, 1], F32)
        nc.vector.tensor_scalar(
            out=negated[:], in0=listed_scores[:], scalar1=-1.0, scalar2=0.0,
            op0=ALU.mult, op1=ALU.min, accum_out=neg_shift[:],
        )
        expo = sb.tile([P, SLOTS], F32)
        expo_sum = sb.tile([P, 1], F32)
        shrink = sb.tile([P, 1], F32)
        nc.scalar.activation(
            out=expo[:], in_=listed_scores[:], func=ACT.Exp, bias=neg_shift[:], accum_out=expo_sum[:]
        )
        nc.scalar.activation(out=shrink[:], in_=neg_shift[:], func=ACT.Exp)

        banks = []
        for n, width in enumerate(VALS_CHUNKS):
            grouped = sb.tile([P, width, PACK], BF16, name="vals_grouped%d" % n, align_bytes=64)
            raw = vals_raw[n]
            for lo in range(0, VECTOR_COLS[n], Q):
                interleave(nc.vector.tensor_copy, grouped[:, lo : lo + Q, :], raw[:, :, lo : lo + Q])
            interleave(scalar_copy, grouped[:, VECTOR_COLS[n] :, :], raw[:, :, VECTOR_COLS[n] :])
            codes, scales = quantize(nc, sb, "vals%d" % n, grouped, width, QUANT_COLS[n])
            bank = psum.tile([P, width], F32, name="prod_bank%d" % n)
            for lo in range(0, width, 256):
                cols = slice(lo, min(lo + 256, width))
                nc.tensor.matmul_mx(
                    out=bank[:, cols],
                    lhsT=gout_codes[:].bitcast(FP8X4),
                    lhsT_scale=gout_scales[:],
                    rhs=codes[:, cols].bitcast(FP8X4),
                    rhs_scale=scales[:, cols],
                    start=True,
                    stop=True,
                )
            banks.append(bank)

        prods = sb.tile([P, T], F32, tag="raw%d" % (len(VALS_CHUNKS) - 1))
        for n, width in enumerate(VALS_CHUNKS):
            copy = nc.vector.tensor_copy if n == len(banks) - 2 else scalar_copy
            copy(out=prods[:, starts[n] : starts[n] + width], in_=banks[n][:])

        norm = sb.tile([P, 1], F32)
        nc.vector.tensor_scalar(
            out=norm[:], in0=zp_col[:], scalar1=shrink[:], scalar2=expo_sum[:], op0=ALU.mult, op1=ALU.add
        )
        inv_norm = sb.tile([P, 1], F32)
        nc.vector.reciprocal(out=inv_norm[:], in_=norm[:])
        listed_prods = sb.tile([P, SLOTS], F32)
        nc.vector.tensor_copy(listed_prods[:], prods[:].indirect(offsets[:]))
        prob = sb.tile([P, SLOTS], F32)
        nc.scalar.activation(out=prob[:], in_=expo[:], func=ACT.Copy, scale=inv_norm[:])
        prefix_mean = sb.tile([P, 1], F32)
        nc.vector.tensor_scalar(
            out=prefix_mean[:], in0=cp_col[:], scalar1=shrink[:], scalar2=inv_norm[:],
            op0=ALU.mult, op1=ALU.mult,
        )
        weighted = sb.tile([P, SLOTS], F32)
        suffix_mean = sb.tile([P, 1], F32)
        nc.vector.scalar_tensor_tensor(
            out=weighted[:], in0=listed_prods[:], scalar=inv_norm[:], in1=expo[:],
            op0=ALU.mult, op1=ALU.mult, accum_out=suffix_mean[:],
        )
        centred = sb.tile([P, SLOTS], F32)
        nc.vector.tensor_scalar(
            out=centred[:], in0=listed_prods[:], scalar1=suffix_mean[:], scalar2=prefix_mean[:],
            op0=ALU.subtract, op1=ALU.subtract,
        )
        nc.vector.tensor_tensor(placed[:].indirect(offsets[:]), centred[:], prob[:], ALU.mult)

        result = sb.tile([P, T], F32)
        for n, width in enumerate(STORE_CHUNKS):
            cols = slice(sum(STORE_CHUNKS[:n]), sum(STORE_CHUNKS[:n]) + width)
            nc.vector.scalar_tensor_tensor(
                out=result[:, cols], in0=placed[:, cols], scalar=1024.0, in1=old_sb[:, cols],
                op0=ALU.mult, op1=ALU.add,
            )
            nc.sync.dma_start(out=out[:, cols], in_=result[:, cols])
